import numpy as np
import ml_dtypes


def mxq(x, axis, fmt="e4m3"):
    dtype, down = {"e4m3": (ml_dtypes.float8_e4m3fn, 7), "e5m2": (ml_dtypes.float8_e5m2, 14)}[fmt]
    v = np.moveaxis(np.asarray(x, np.float32).astype(ml_dtypes.bfloat16).astype(np.float64), axis, -1)
    blocks = v.reshape(v.shape[:-1] + (-1, 32))
    amax = np.abs(blocks).max(-1, keepdims=True)
    byte = np.maximum(np.where(amax > 0, np.frexp(amax)[1] - 1 + 127, 0) - down, 1)
    scale = np.exp2(byte - 127.0)
    codes = (blocks / scale).astype(np.float32).astype(dtype).astype(np.float64)
    return np.moveaxis((codes * scale).reshape(v.shape), -1, axis)


WIDE = False


def mx_kscale(k):
    if not WIDE:
        return np.ones(k)
    levels = np.array([10, -10, 5, -5, 0])
    if k % 512:
        return np.exp2(np.random.permutation(np.resize(levels, k // 32))).repeat(32)
    a = np.empty((k // 512, 16))
    for p in range(k // 512):
        a[p, :8] = np.random.permutation(np.resize(levels, 8))
        for g in range(8):
            far = levels[np.abs(levels - a[p, g]) >= 10]
            a[p, g + 8] = far[np.random.randint(len(far))]
    return np.exp2(a.ravel()).repeat(32)


def f64(x):
    return np.asarray(x).astype(np.float64)


def striped(idx):
    return np.tile(np.asarray(idx).reshape(-1, 16).T, (8, 1)).astype(np.uint16)


def unstriped(offs):
    return offs[:16].T.reshape(-1).astype(np.int64)


E2M1 = np.array([0.0, 0.5, 1.0, 1.5, 2.0, 3.0, 4.0, 6.0, -0.0, -0.5, -1.0, -1.5, -2.0, -3.0, -4.0, -6.0])


def pack_weight(w, fmt):
    k, n = w.shape
    w = f64(np.asarray(w, np.float32).astype(ml_dtypes.bfloat16)).reshape(k // 32, 32, n)
    amax = np.abs(w).max(1)
    if fmt == "e4m3":
        byte = np.frexp(amax)[1] - 1 + 127 - 7
    else:
        mant, ex = np.frexp(amax / 6.0)
        byte = np.where(mant > 0.5, ex, ex - 1) + 127
    byte = np.clip(np.where(amax > 0, byte, 1), 1, 254)
    scaled = (w * np.exp2(127.0 - byte)[:, None, :]).reshape(k, n).astype(np.float32)
    by_word = np.ascontiguousarray(scaled.reshape(k // 512, 128, 4, n).transpose(0, 1, 3, 2))
    if fmt == "e4m3":
        words = by_word.astype(ml_dtypes.float8_e4m3fn).view(np.uint8)
    else:
        c = by_word.astype(ml_dtypes.float4_e2m1fn).view(np.uint8) & 0xF
        words = (c[..., 0::2] | (c[..., 1::2] << 4)).reshape(k // 512, 128, 2 * n)
    return np.ascontiguousarray(words), np.ascontiguousarray(byte.astype(np.uint8).reshape(k // 512, 16, n))


def unpack_weight(words, scales, fmt):
    g, _, n = scales.shape
    words = np.ascontiguousarray(words).reshape(g, 128, n, -1)
    if fmt == "e4m3":
        vals = words.view(ml_dtypes.float8_e4m3fn).astype(np.float64)
    else:
        nib = np.empty((g, 128, n, 4), np.uint8)
        nib[..., 0::2] = words & 0xF
        nib[..., 1::2] = words >> 4
        vals = E2M1[nib]
    vals = vals * np.repeat(np.exp2(scales.astype(np.float64) - 127.0), 8, axis=1)[..., None]
    return vals.transpose(0, 1, 3, 2).reshape(g * 512, n)


B, N, T, D, NQ = 1, 512, 4096, 1024, 128


def setup_inputs():
    n = np.random.standard_normal
    idx = np.sort(np.random.permutation(T)[:B * N].reshape(B, N), axis=1).reshape(-1)
    s = mx_kscale(D)[:, None]
    kp = pack_weight(n((D, T)) / s, "e2m1")
    return {
        "qT": (n((B, D, NQ)) * s * (1.00 / np.sqrt(D))).astype(np.float32),
        "k_words": np.ascontiguousarray(kp[0].reshape(1, 2, 128, T, 2).transpose(0, 2, 3, 1, 4)).reshape(1, 128, T, 4),
        "k_scales": kp[1],
        "ls": (np.random.uniform(8.5, 9.0, (B, NQ, 1))).astype(np.float32),
        "pd": (np.exp(0.7 * n((B, NQ, N)) - 8.8)).astype(np.float32),
        "offs": striped(idx),
    }


def reference(qT, k_words, k_scales, ls, pd, offs):
    idx = unstriped(offs)
    pick = lambda x, which: x[:, which].reshape(x.shape[0], B, -1).transpose(1, 0, 2)
    k = unpack_weight(k_words.reshape(1, 128, T, 2, 2).transpose(0, 3, 1, 2, 4).reshape(2, 128, 2 * T), k_scales, "e2m1")
    kg = pick(k, idx)
    qq = mxq(f64(qT), 1, "e4m3")
    a = qq.transpose(0, 2, 1) @ kg
    y = np.minimum(np.exp(a - f64(ls)) / f64(pd), 1.0)
    return y

@@ -1,0 +1,113 @@
+from contextlib import ExitStack
+
+import concourse.mybir as mybir
+
+D, T, N, NQ = 1024, 4096, 512, 128
+FLOPS = 2 * NQ * N * D
+
+F32 = mybir.dt.float32
+BF16 = mybir.dt.bfloat16
+I32 = mybir.dt.int32
+U32 = mybir.dt.uint32
+U16 = mybir.dt.uint16
+U8 = mybir.dt.uint8
+FP8X4 = mybir.dt.float8_e4m3fn_x4
+FP4X4 = mybir.dt.float4_e2m1fn_x4
+ALU = mybir.AluOpType
+ACT = mybir.ActivationFunctionType
+
+P = 128
+PACK = 4
+K_PASS = P * PACK
+PASSES = D // K_PASS
+CHUNK = 128
+CHUNKS = N // CHUNK
+STORE = 256
+
+
+def tile_attend_accept_srt_kernel(tc, qT, k_words, k_scales, ls, pd, offs, out):
+    nc = tc.nc
+    with ExitStack() as ctx:
+        keep = ctx.enter_context(tc.tile_pool(name="keep", bufs=1))
+        psum = ctx.enter_context(tc.psum_pool(name="psum", bufs=1))
+
+        offsets = keep.tile([P, N // 16], U16, name="offsets")
+        words = keep.tile([P, T], U32, name="words")
+        rows = keep.tile([P, PASSES * T // 4], I32, name="rows")
+        plane = keep.tile([P, PASSES * N // 4], I32, name="plane", align_bytes=64)
+        pd_sb = keep.tile([P, N], F32, name="pd_sb")
+        ls_sb = keep.tile([P, 1], F32, name="ls_sb")
+        q_raw = [keep.tile([P, PACK, NQ], F32, name="q_raw%d" % o) for o in range(PASSES)]
+
+        nc.scalar.dma_start(out=words[:].bitcast(I32), in_=k_words[0].rearrange("p t b -> p (t b)").bitcast(I32))
+        for o in range(PASSES):
+            nc.scalar.dma_start(out=q_raw[o][:], in_=qT[0, o * K_PASS : (o + 1) * K_PASS, :].rearrange("(p j) w -> p j w", j=PACK))
+        nc.sync.dma_start(offsets[:], offs)
+        nc.sync.dma_start(out=pd_sb[:], in_=pd[0])
+        nc.gpsimd.dma_start(out=ls_sb[:], in_=ls[0])
+
+        nc.vector.memset(rows[:], 0)
+        nc.vector.memset(plane[:], 0)
+        nc.sync.dma_start(
+            out=rows[0:P:8, :].rearrange("f (o t) -> f o t", o=PASSES),
+            in_=k_scales.bitcast(I32).rearrange("o f t -> f o t"),
+        )
+
+        log_pd = keep.tile([P, N], F32, name="log_pd")
+        nc.scalar.activation(out=log_pd[:], in_=pd_sb[:], func=ACT.Ln)
+        warm = keep.tile([P, 1], F32, name="warm")
+        nc.scalar.activation(out=warm[:], in_=log_pd[:, 0:1], func=ACT.Exp)
+
+        picked_rows = keep.tile([P, PASSES * N], U8, name="picked_rows")
+        for o in range(PASSES):
+            nc.vector.tensor_copy(
+                picked_rows[:, o * N : (o + 1) * N],
+                rows[:].bitcast(U8)[:, o * T : (o + 1) * T].indirect(offsets[:]),
+            )
+        for quad in range(4):
+            nc.sync.dma_start(
+                out=plane[32 * quad : 32 * quad + 4, :],
+                in_=picked_rows[32 * quad : 32 * quad + 32 : 8, :].bitcast(I32),
+            )
+        k_scale = plane[:].bitcast(U8)
+
+        picked_words = keep.tile([P, N], U32, name="picked_words")
+        nc.vector.tensor_copy(picked_words[:], words[:].indirect(offsets[:]))
+        halves = picked_words[:].bitcast(U16).rearrange("p (n o) -> p o n", o=PASSES)
+
+        banks = [psum.tile([P, CHUNK], F32, name="bank%d" % c) for c in range(CHUNKS)]
+        for o in range(PASSES):
+            k_codes = keep.tile([P, 2 * N], U8, name="k_codes%d" % o, align_bytes=64)
+            nc.vector.tensor_copy(out=k_codes[:].bitcast(U16), in_=halves[:, o, :])
+            q_bf = keep.tile([P, NQ, PACK], BF16, name="q_bf%d" % o, align_bytes=64)
+            nc.scalar.copy(out=q_bf[:], in_=q_raw[o][:].rearrange("p j w -> p w j"))
+            q_codes = keep.tile([P, NQ], U32, name="q_codes%d" % o, align_bytes=64)
+            q_scale = keep.tile([P, NQ], U8, name="q_scale%d" % o, align_bytes=64)
+            nc.vector.quantize_mx(
+                out=q_codes[:].bitcast(FP8X4), scales=q_scale[:], in_=q_bf[:].rearrange("p w j -> p (w j)")
+            )
+            for c in range(CHUNKS):
+                nc.tensor.matmul_mx(
+                    out=banks[c][:],
+                    lhsT=q_codes[:].bitcast(FP8X4),
+                    lhsT_scale=q_scale[:],
+                    rhs=k_codes[:, 2 * c * CHUNK : 2 * (c + 1) * CHUNK].bitcast(FP4X4),
+                    rhs_scale=k_scale[:, o * N + c * CHUNK : o * N + (c + 1) * CHUNK],
+                    start=(o == 0),
+                    stop=(o == PASSES - 1),
+                )
+
+        log_ratio = keep.tile([P, N], F32, name="log_ratio")
+        ratio = keep.tile([P, N], F32, name="ratio")
+        result = keep.tile([P, N], F32, name="result")
+        for c in range(CHUNKS):
+            cols = slice(c * CHUNK, (c + 1) * CHUNK)
+            nc.vector.scalar_tensor_tensor(
+                out=log_ratio[:, cols], in0=banks[c][:], scalar=ls_sb[:], in1=log_pd[:, cols],
+                op0=ALU.subtract, op1=ALU.subtract,
+            )
+            nc.scalar.activation(out=ratio[:, cols], in_=log_ratio[:, cols], func=ACT.Exp)
+        for s in range(N // STORE):
+            cols = slice(s * STORE, (s + 1) * STORE)
+            nc.vector.tensor_scalar_min(out=result[:, cols], in0=ratio[:, cols], scalar1=1.0)
+            nc.sync.dma_start(out=out[0, :, cols], in_=result[:, cols])

@@ -22,7 +22,7 @@ K_PASS = P * PACK
 PASSES = D // K_PASS
 CHUNK = 128
 CHUNKS = N // CHUNK
-STORE = 256
+STORES = ((0, 256), (256, 512))
 
 
 def tile_attend_accept_srt_kernel(tc, qT, k_words, k_scales, ls, pd, offs, out):
@@ -33,81 +33,104 @@ def tile_attend_accept_srt_kernel(tc, qT, k_words, k_scales, ls, pd, offs, out):
 
         offsets = keep.tile([P, N // 16], U16, name="offsets")
         words = keep.tile([P, T], U32, name="words")
-        rows = keep.tile([P, PASSES * T // 4], I32, name="rows")
-        plane = keep.tile([P, PASSES * N // 4], I32, name="plane", align_bytes=64)
+        rows = keep.tile([P, T // 4], I32, name="rows")
+        planes = [keep.tile([P, N // 4], I32, name="plane%d" % o, align_bytes=64) for o in range(PASSES)]
         pd_sb = keep.tile([P, N], F32, name="pd_sb")
         ls_sb = keep.tile([P, 1], F32, name="ls_sb")
         q_raw = [keep.tile([P, PACK, NQ], F32, name="q_raw%d" % o) for o in range(PASSES)]
 
-        nc.scalar.dma_start(out=words[:].bitcast(I32), in_=k_words[0].rearrange("p t b -> p (t b)").bitcast(I32))
-        for o in range(PASSES):
-            nc.scalar.dma_start(out=q_raw[o][:], in_=qT[0, o * K_PASS : (o + 1) * K_PASS, :].rearrange("(p j) w -> p j w", j=PACK))
-        nc.sync.dma_start(offsets[:], offs)
-        nc.sync.dma_start(out=pd_sb[:], in_=pd[0])
-        nc.gpsimd.dma_start(out=ls_sb[:], in_=ls[0])
+        def q_rows(o):
+            return qT[0, o * K_PASS : (o + 1) * K_PASS, :].rearrange("(p j) w -> p j w", j=PACK)
 
-        nc.vector.memset(rows[:], 0)
-        nc.vector.memset(plane[:], 0)
-        nc.sync.dma_start(
-            out=rows[0:P:8, :].rearrange("f (o t) -> f o t", o=PASSES),
-            in_=k_scales.bitcast(I32).rearrange("o f t -> f o t"),
-        )
+        nc.scalar.dma_start(out=ls_sb[:], in_=ls[0])
+        nc.scalar.dma_start(out=pd_sb[:], in_=pd[0])
+        nc.sync.dma_start(out=rows[0:32, :], in_=k_scales.bitcast(I32).rearrange("o f t -> (o f) t"))
+        nc.sync.dma_start(offsets[:], offs)
+        nc.sync.dma_start(out=words[:].bitcast(I32), in_=k_words[0].rearrange("p t b -> p (t b)").bitcast(I32))
+        nc.sync.dma_start(out=q_raw[0][:], in_=q_rows(0))
+        nc.sync.dma_start(out=q_raw[1][:], in_=q_rows(1))
+        nc.vector.memset(rows[32:64, :], 0)
+        nc.vector.memset(rows[64:128, :], 0)
+        for o in range(PASSES):
+            nc.vector.memset(planes[o][:], 0)
 
         log_pd = keep.tile([P, N], F32, name="log_pd")
         nc.scalar.activation(out=log_pd[:], in_=pd_sb[:], func=ACT.Ln)
-        warm = keep.tile([P, 1], F32, name="warm")
-        nc.scalar.activation(out=warm[:], in_=log_pd[:, 0:1], func=ACT.Exp)
 
-        picked_rows = keep.tile([P, PASSES * N], U8, name="picked_rows")
-        for o in range(PASSES):
-            nc.vector.tensor_copy(
-                picked_rows[:, o * N : (o + 1) * N],
-                rows[:].bitcast(U8)[:, o * T : (o + 1) * T].indirect(offsets[:]),
+        q_bf = [keep.tile([P, NQ, PACK], BF16, name="q_bf%d" % o, tag="q_bf%d" % o, align_bytes=64) for o in range(PASSES)]
+        q_codes = [keep.tile([P, NQ], U32, name="q_codes%d" % o, align_bytes=64) for o in range(PASSES)]
+        q_scale = [keep.tile([P, NQ], U8, name="q_scale%d" % o, align_bytes=64) for o in range(PASSES)]
+
+        def round_q(o):
+            nc.scalar.copy(out=q_bf[o][:], in_=q_raw[o][:].rearrange("p j w -> p w j"))
+
+        def quantize_q(o):
+            nc.vector.quantize_mx(
+                out=q_codes[o][:].bitcast(FP8X4), scales=q_scale[o][:], in_=q_bf[o][:].rearrange("p w j -> p (w j)")
             )
-        for quad in range(4):
+
+        picked_rows = keep.tile([P, N], U8, name="picked_rows")
+        nc.vector.tensor_copy(picked_rows[:], rows[:].bitcast(U8).indirect(offsets[:]))
+        nc.vector.tensor_copy(out=planes[0][0:32, :], in_=picked_rows[0:32, :].bitcast(I32))
+        for move in range(1, 8):
+            o, quad = divmod(move, 4)
             nc.sync.dma_start(
-                out=plane[32 * quad : 32 * quad + 4, :],
-                in_=picked_rows[32 * quad : 32 * quad + 32 : 8, :].bitcast(I32),
+                out=planes[o][32 * quad : 32 * quad + 4, :],
+                in_=picked_rows[4 * move : 4 * move + 4, :].bitcast(I32),
             )
-        k_scale = plane[:].bitcast(U8)
+        inv_pd = keep.tile([P, CHUNKS // 2, CHUNK], F32, name="inv_pd")
+        even_chunks = log_pd[:].rearrange("p (c two n) -> p c two n", two=2, n=CHUNK)[:, :, 0, :]
+        nc.scalar.activation(out=inv_pd[:], in_=even_chunks, func=ACT.Exp, scale=-1.0)
+        neg_ls = keep.tile([P, 1], F32, name="neg_ls")
+        nc.gpsimd.tensor_scalar_mul(out=neg_ls[:], in0=ls_sb[:], scalar1=-1.0)
+        round_q(0)
+        round_q(1)
 
         picked_words = keep.tile([P, N], U32, name="picked_words")
         nc.vector.tensor_copy(picked_words[:], words[:].indirect(offsets[:]))
         halves = picked_words[:].bitcast(U16).rearrange("p (n o) -> p o n", o=PASSES)
 
         banks = [psum.tile([P, CHUNK], F32, name="bank%d" % c) for c in range(CHUNKS)]
+        k_codes = []
+
+        def split(o, first, last):
+            nc.vector.tensor_copy(out=k_codes[o][:].bitcast(U16)[:, first:last], in_=halves[:, o, first:last])
+
         for o in range(PASSES):
-            k_codes = keep.tile([P, 2 * N], U8, name="k_codes%d" % o, align_bytes=64)
-            nc.vector.tensor_copy(out=k_codes[:].bitcast(U16), in_=halves[:, o, :])
-            q_bf = keep.tile([P, NQ, PACK], BF16, name="q_bf%d" % o, align_bytes=64)
-            nc.scalar.copy(out=q_bf[:], in_=q_raw[o][:].rearrange("p j w -> p w j"))
-            q_codes = keep.tile([P, NQ], U32, name="q_codes%d" % o, align_bytes=64)
-            q_scale = keep.tile([P, NQ], U8, name="q_scale%d" % o, align_bytes=64)
-            nc.vector.quantize_mx(
-                out=q_codes[:].bitcast(FP8X4), scales=q_scale[:], in_=q_bf[:].rearrange("p w j -> p (w j)")
-            )
+            quantize_q(o)
+            k_codes.append(keep.tile([P, 2 * N], U8, name="k_codes%d" % o, tag=("k_codes0", "q_bf0")[o], align_bytes=64))
+            split(o, 0, N)
             for c in range(CHUNKS):
                 nc.tensor.matmul_mx(
                     out=banks[c][:],
-                    lhsT=q_codes[:].bitcast(FP8X4),
-                    lhsT_scale=q_scale[:],
-                    rhs=k_codes[:, 2 * c * CHUNK : 2 * (c + 1) * CHUNK].bitcast(FP4X4),
-                    rhs_scale=k_scale[:, o * N + c * CHUNK : o * N + (c + 1) * CHUNK],
+                    lhsT=q_codes[o][:].bitcast(FP8X4),
+                    lhsT_scale=q_scale[o][:],
+                    rhs=k_codes[o][:, 2 * c * CHUNK : 2 * (c + 1) * CHUNK].bitcast(FP4X4),
+                    rhs_scale=planes[o][:].bitcast(U8)[:, c * CHUNK : (c + 1) * CHUNK],
                     start=(o == 0),
                     stop=(o == PASSES - 1),
                 )
 
-        log_ratio = keep.tile([P, N], F32, name="log_ratio")
+        midway = keep.tile([P, N], F32, name="midway")
         ratio = keep.tile([P, N], F32, name="ratio")
         result = keep.tile([P, N], F32, name="result")
         for c in range(CHUNKS):
             cols = slice(c * CHUNK, (c + 1) * CHUNK)
-            nc.vector.scalar_tensor_tensor(
-                out=log_ratio[:, cols], in0=banks[c][:], scalar=ls_sb[:], in1=log_pd[:, cols],
-                op0=ALU.subtract, op1=ALU.subtract,
-            )
-            nc.scalar.activation(out=ratio[:, cols], in_=log_ratio[:, cols], func=ACT.Exp)
-        for s in range(N // STORE):
-            cols = slice(s * STORE, (s + 1) * STORE)
+            if c % 2 == 0:
+                nc.scalar.activation(out=midway[:, cols], in_=banks[c][:], func=ACT.Exp, bias=neg_ls[:])
+            else:
+                nc.vector.scalar_tensor_tensor(
+                    out=midway[:, cols], in0=banks[c][:], scalar=neg_ls[:], in1=log_pd[:, cols],
+                    op0=ALU.add, op1=ALU.subtract,
+                )
+        for c in range(CHUNKS):
+            cols = slice(c * CHUNK, (c + 1) * CHUNK)
+            if c % 2 == 0:
+                nc.vector.tensor_tensor(out=ratio[:, cols], in0=midway[:, cols], in1=inv_pd[:, c // 2, :], op=ALU.mult)
+            else:
+                nc.scalar.activation(out=ratio[:, cols], in_=midway[:, cols], func=ACT.Exp)
+        for first, last in STORES:
+            cols = slice(first, last)
             nc.vector.tensor_scalar_min(out=result[:, cols], in0=ratio[:, cols], scalar1=1.0)
-            nc.sync.dma_start(out=out[0, :, cols], in_=result[:, cols])
+            queue = nc.scalar if last == N else nc.sync
+            queue.dma_start(out=out[0, :, cols], in_=result[:, cols])

@@ -36,16 +36,17 @@ def tile_attend_accept_srt_kernel(tc, qT, k_words, k_scales, ls, pd, offs, out):
         rows = keep.tile([P, T // 4], I32, name="rows")
         planes = [keep.tile([P, N // 4], I32, name="plane%d" % o, align_bytes=64) for o in range(PASSES)]
         pd_sb = keep.tile([P, N], F32, name="pd_sb")
-        ls_sb = keep.tile([P, 1], F32, name="ls_sb")
+        ls_rows = keep.tile([P, 32], F32, name="ls_rows", align_bytes=64)
         q_raw = [keep.tile([P, PACK, NQ], F32, name="q_raw%d" % o) for o in range(PASSES)]
 
         def q_rows(o):
             return qT[0, o * K_PASS : (o + 1) * K_PASS, :].rearrange("(p j) w -> p j w", j=PACK)
 
-        nc.scalar.dma_start(out=ls_sb[:], in_=ls[0])
+        nc.vector.memset(ls_rows[:], 0.0)
         nc.scalar.dma_start(out=pd_sb[:], in_=pd[0])
         nc.sync.dma_start(out=rows[0:32, :], in_=k_scales.bitcast(I32).rearrange("o f t -> (o f) t"))
         nc.sync.dma_start(offsets[:], offs)
+        nc.sync.dma_start(out=ls_rows[0:P:32, :], in_=ls[0].rearrange("(g i) one -> g (i one)", i=32))
         nc.sync.dma_start(out=words[:].bitcast(I32), in_=k_words[0].rearrange("p t b -> p (t b)").bitcast(I32))
         nc.sync.dma_start(out=q_raw[0][:], in_=q_rows(0))
         nc.sync.dma_start(out=q_raw[1][:], in_=q_rows(1))
@@ -62,7 +63,10 @@ def tile_attend_accept_srt_kernel(tc, qT, k_words, k_scales, ls, pd, offs, out):
         q_scale = [keep.tile([P, NQ], U8, name="q_scale%d" % o, align_bytes=64) for o in range(PASSES)]
 
         def round_q(o):
-            nc.scalar.copy(out=q_bf[o][:], in_=q_raw[o][:].rearrange("p j w -> p w j"))
+            nc.scalar.copy(
+                out=q_bf[o][:].rearrange("p (c i) j -> p c j i", i=4),
+                in_=q_raw[o][:].rearrange("p j (c i) -> p c j i", i=4),
+            )
 
         def quantize_q(o):
             nc.vector.quantize_mx(
@@ -74,7 +78,8 @@ def tile_attend_accept_srt_kernel(tc, qT, k_words, k_scales, ls, pd, offs, out):
         nc.vector.tensor_copy(out=planes[0][0:32, :], in_=picked_rows[0:32, :].bitcast(I32))
         for move in range(1, 8):
             o, quad = divmod(move, 4)
-            nc.sync.dma_start(
+            queue = nc.sync if move < 6 else nc.gpsimd
+            queue.dma_start(
                 out=planes[o][32 * quad : 32 * quad + 4, :],
                 in_=picked_rows[4 * move : 4 * move + 4, :].bitcast(I32),
             )
@@ -82,7 +87,9 @@ def tile_attend_accept_srt_kernel(tc, qT, k_words, k_scales, ls, pd, offs, out):
         even_chunks = log_pd[:].rearrange("p (c two n) -> p c two n", two=2, n=CHUNK)[:, :, 0, :]
         nc.scalar.activation(out=inv_pd[:], in_=even_chunks, func=ACT.Exp, scale=-1.0)
         neg_ls = keep.tile([P, 1], F32, name="neg_ls")
-        nc.gpsimd.tensor_scalar_mul(out=neg_ls[:], in0=ls_sb[:], scalar1=-1.0)
+        ls_cols = keep.tile([P, 32], F32, name="ls_cols", align_bytes=64)
+        nc.vector.transpose(out=ls_cols[:], in_=ls_rows[:])
+        nc.vector.tensor_scalar_mul(out=neg_ls[:], in0=ls_cols[:, 0:1], scalar1=-1.0)
         round_q(0)
         round_q(1)
 

@@ -22,7 +22,6 @@ K_PASS = P * PACK
 PASSES = D // K_PASS
 CHUNK = 128
 CHUNKS = N // CHUNK
-STORES = ((0, 256), (256, 512))
 
 
 def tile_attend_accept_srt_kernel(tc, qT, k_words, k_scales, ls, pd, offs, out):
@@ -34,17 +33,17 @@ def tile_attend_accept_srt_kernel(tc, qT, k_words, k_scales, ls, pd, offs, out):
         offsets = keep.tile([P, N // 16], U16, name="offsets")
         words = keep.tile([P, T], U32, name="words")
         rows = keep.tile([P, T // 4], I32, name="rows")
-        planes = [keep.tile([P, N // 4], I32, name="plane%d" % o, align_bytes=64) for o in range(PASSES)]
+        planes = keep.tile([P, PASSES * N // 4], I32, name="planes", align_bytes=64)
         pd_sb = keep.tile([P, N], F32, name="pd_sb")
         ls_rows = keep.tile([P, 32], F32, name="ls_rows", align_bytes=64)
-        q_raw = [keep.tile([P, PACK, NQ], F32, name="q_raw%d" % o) for o in range(PASSES)]
+        q_raw = [keep.tile([P, PACK, NQ], F32, name="q_raw%d" % o, tag="q_raw%d" % o, align_bytes=64) for o in range(PASSES)]
 
         def q_rows(o):
             return qT[0, o * K_PASS : (o + 1) * K_PASS, :].rearrange("(p j) w -> p j w", j=PACK)
 
         nc.vector.memset(ls_rows[:], 0.0)
         nc.scalar.dma_start(out=pd_sb[:], in_=pd[0])
-        nc.sync.dma_start(out=rows[0:32, :], in_=k_scales.bitcast(I32).rearrange("o f t -> (o f) t"))
+        nc.sync.dma_start(out=rows[0:32, :], in_=k_scales.bitcast(I32).rearrange("o f t -> f o t"))
         nc.sync.dma_start(offsets[:], offs)
         nc.sync.dma_start(out=ls_rows[0:P:32, :], in_=ls[0].rearrange("(g i) one -> g (i one)", i=32))
         nc.sync.dma_start(out=words[:].bitcast(I32), in_=k_words[0].rearrange("p t b -> p (t b)").bitcast(I32))
@@ -52,8 +51,7 @@ def tile_attend_accept_srt_kernel(tc, qT, k_words, k_scales, ls, pd, offs, out):
         nc.sync.dma_start(out=q_raw[1][:], in_=q_rows(1))
         nc.vector.memset(rows[32:64, :], 0)
         nc.vector.memset(rows[64:128, :], 0)
-        for o in range(PASSES):
-            nc.vector.memset(planes[o][:], 0)
+        nc.vector.memset(planes[:], 0)
 
         log_pd = keep.tile([P, N], F32, name="log_pd")
         nc.scalar.activation(out=log_pd[:], in_=pd_sb[:], func=ACT.Ln)
@@ -75,17 +73,13 @@ def tile_attend_accept_srt_kernel(tc, qT, k_words, k_scales, ls, pd, offs, out):
 
         picked_rows = keep.tile([P, N], U8, name="picked_rows")
         nc.vector.tensor_copy(picked_rows[:], rows[:].bitcast(U8).indirect(offsets[:]))
-        nc.vector.tensor_copy(out=planes[0][0:32, :], in_=picked_rows[0:32, :].bitcast(I32))
-        for move in range(1, 8):
-            o, quad = divmod(move, 4)
-            queue = nc.sync if move < 6 else nc.gpsimd
-            queue.dma_start(
-                out=planes[o][32 * quad : 32 * quad + 4, :],
-                in_=picked_rows[4 * move : 4 * move + 4, :].bitcast(I32),
+        for quad in range(4):
+            nc.sync.dma_start(
+                out=planes[32 * quad : 32 * quad + 4, :],
+                in_=picked_rows[8 * quad : 8 * quad + 8, :].bitcast(I32),
             )
-        inv_pd = keep.tile([P, CHUNKS // 2, CHUNK], F32, name="inv_pd")
-        even_chunks = log_pd[:].rearrange("p (c two n) -> p c two n", two=2, n=CHUNK)[:, :, 0, :]
-        nc.scalar.activation(out=inv_pd[:], in_=even_chunks, func=ACT.Exp, scale=-1.0)
+        inv_pd = keep.tile([P, CHUNK], F32, name="inv_pd")
+        nc.scalar.activation(out=inv_pd[:], in_=log_pd[:, 0:CHUNK], func=ACT.Exp, scale=-1.0)
         neg_ls = keep.tile([P, 1], F32, name="neg_ls")
         ls_cols = keep.tile([P, 32], F32, name="ls_cols", align_bytes=64)
         nc.vector.transpose(out=ls_cols[:], in_=ls_rows[:])
@@ -98,46 +92,55 @@ def tile_attend_accept_srt_kernel(tc, qT, k_words, k_scales, ls, pd, offs, out):
         halves = picked_words[:].bitcast(U16).rearrange("p (n o) -> p o n", o=PASSES)
 
         banks = [psum.tile([P, CHUNK], F32, name="bank%d" % c) for c in range(CHUNKS)]
-        k_codes = []
 
-        def split(o, first, last):
-            nc.vector.tensor_copy(out=k_codes[o][:].bitcast(U16)[:, first:last], in_=halves[:, o, first:last])
+        def codes_tile(o, first, last, tag):
+            return keep.tile([P, 2 * (last - first)], U8, name="k_codes%d_%d" % (o, first), tag=tag, align_bytes=64)
 
-        for o in range(PASSES):
-            quantize_q(o)
-            k_codes.append(keep.tile([P, 2 * N], U8, name="k_codes%d" % o, tag=("k_codes0", "q_bf0")[o], align_bytes=64))
-            split(o, 0, N)
-            for c in range(CHUNKS):
-                nc.tensor.matmul_mx(
-                    out=banks[c][:],
-                    lhsT=q_codes[o][:].bitcast(FP8X4),
-                    lhsT_scale=q_scale[o][:],
-                    rhs=k_codes[o][:, 2 * c * CHUNK : 2 * (c + 1) * CHUNK].bitcast(FP4X4),
-                    rhs_scale=planes[o][:].bitcast(U8)[:, c * CHUNK : (c + 1) * CHUNK],
-                    start=(o == 0),
-                    stop=(o == PASSES - 1),
-                )
+        def split(o, first, last, codes):
+            nc.vector.tensor_copy(out=codes.bitcast(U16), in_=halves[:, o, first:last])
 
-        midway = keep.tile([P, N], F32, name="midway")
-        ratio = keep.tile([P, N], F32, name="ratio")
-        result = keep.tile([P, N], F32, name="result")
-        for c in range(CHUNKS):
-            cols = slice(c * CHUNK, (c + 1) * CHUNK)
-            if c % 2 == 0:
-                nc.scalar.activation(out=midway[:, cols], in_=banks[c][:], func=ACT.Exp, bias=neg_ls[:])
-            else:
-                nc.vector.scalar_tensor_tensor(
-                    out=midway[:, cols], in0=banks[c][:], scalar=neg_ls[:], in1=log_pd[:, cols],
-                    op0=ALU.add, op1=ALU.subtract,
-                )
-        for c in range(CHUNKS):
-            cols = slice(c * CHUNK, (c + 1) * CHUNK)
-            if c % 2 == 0:
-                nc.vector.tensor_tensor(out=ratio[:, cols], in0=midway[:, cols], in1=inv_pd[:, c // 2, :], op=ALU.mult)
-            else:
-                nc.scalar.activation(out=ratio[:, cols], in_=midway[:, cols], func=ACT.Exp)
-        for first, last in STORES:
-            cols = slice(first, last)
-            nc.vector.tensor_scalar_min(out=result[:, cols], in0=ratio[:, cols], scalar1=1.0)
-            queue = nc.scalar if last == N else nc.sync
-            queue.dma_start(out=out[0, :, cols], in_=result[:, cols])
+        def multiply(o, c, codes):
+            nc.tensor.matmul_mx(
+                out=banks[c][:],
+                lhsT=q_codes[o][:].bitcast(FP8X4),
+                lhsT_scale=q_scale[o][:],
+                rhs=codes.bitcast(FP4X4),
+                rhs_scale=planes[:].bitcast(U8)[:, o * N + c * CHUNK : o * N + (c + 1) * CHUNK],
+                start=(o == 0),
+                stop=(o == PASSES - 1),
+            )
+
+        head = codes_tile(0, 0, CHUNK, "k_head")
+        split(0, 0, CHUNK, head[:])
+        quantize_q(0)
+        multiply(0, 0, head[:])
+        middle = codes_tile(0, CHUNK, N + CHUNK, "q_raw0")
+        split(0, CHUNK, 2 * CHUNK, middle[:, 0 : 2 * CHUNK])
+        split(0, 2 * CHUNK, N, middle[:, 2 * CHUNK : 2 * (N - CHUNK)])
+        for c in range(1, CHUNKS):
+            multiply(0, c, middle[:, 2 * (c - 1) * CHUNK : 2 * c * CHUNK])
+        split(1, 0, CHUNK, middle[:, 2 * (N - CHUNK) : 2 * N])
+        quantize_q(1)
+        multiply(1, 0, middle[:, 2 * (N - CHUNK) : 2 * N])
+        tail = codes_tile(1, CHUNK, N, "q_raw1")
+        split(1, CHUNK, 2 * CHUNK, tail[:, 0 : 2 * CHUNK])
+        split(1, 2 * CHUNK, N, tail[:, 2 * CHUNK : 2 * (N - CHUNK)])
+        for c in range(1, CHUNKS):
+            multiply(1, c, tail[:, 2 * (c - 1) * CHUNK : 2 * c * CHUNK])
+
+        midway = [keep.tile([P, CHUNK], F32, name="midway%d" % c) for c in range(CHUNKS)]
+        ratio = [keep.tile([P, CHUNK], F32, name="ratio%d" % c) for c in range(CHUNKS)]
+        result = [keep.tile([P, CHUNK], F32, name="result%d" % c) for c in range(CHUNKS)]
+        nc.scalar.activation(out=midway[0][:], in_=banks[0][:], func=ACT.Exp, bias=neg_ls[:])
+        for c in range(1, CHUNKS):
+            nc.vector.scalar_tensor_tensor(
+                out=midway[c][:], in0=banks[c][:], scalar=neg_ls[:], in1=log_pd[:, c * CHUNK : (c + 1) * CHUNK],
+                op0=ALU.add, op1=ALU.subtract,
+            )
+        nc.vector.tensor_tensor(out=ratio[0][:], in0=midway[0][:], in1=inv_pd[:], op=ALU.mult)
+        for c in range(1, CHUNKS):
+            nc.scalar.activation(out=ratio[c][:], in_=midway[c][:], func=ACT.Exp)
+        for c in (1, 0, 2, 3):
+            nc.vector.tensor_scalar_min(out=result[c][:], in0=ratio[c][:], scalar1=1.0)
+            queue = nc.scalar if c == CHUNKS - 1 else nc.sync
+            queue.dma_start(out=out[0, :, c * CHUNK : (c + 1) * CHUNK], in_=result[c][:])

@@ -22,6 +22,7 @@ K_PASS = P * PACK
 PASSES = D // K_PASS
 CHUNK = 128
 CHUNKS = N // CHUNK
+T_HEAD = T // 4
 
 
 def tile_attend_accept_srt_kernel(tc, qT, k_words, k_scales, ls, pd, offs, out):
@@ -41,16 +42,17 @@ def tile_attend_accept_srt_kernel(tc, qT, k_words, k_scales, ls, pd, offs, out):
         def q_rows(o):
             return qT[0, o * K_PASS : (o + 1) * K_PASS, :].rearrange("(p j) w -> p j w", j=PACK)
 
+        words_hbm = k_words[0].rearrange("p t b -> p (t b)").bitcast(I32)
         nc.vector.memset(ls_rows[:], 0.0)
+        nc.vector.memset(rows[:], 0)
         nc.scalar.dma_start(out=pd_sb[:], in_=pd[0])
-        nc.sync.dma_start(out=rows[0:32, :], in_=k_scales.bitcast(I32).rearrange("o f t -> f o t"))
+        nc.sync.dma_start(out=rows[0:P:4, :], in_=k_scales.bitcast(I32).rearrange("o f t -> f o t"))
+        nc.sync.dma_start(out=words[:, 0:T_HEAD].bitcast(I32), in_=words_hbm[:, 0:T_HEAD])
         nc.sync.dma_start(offsets[:], offs)
         nc.sync.dma_start(out=ls_rows[0:P:32, :], in_=ls[0].rearrange("(g i) one -> g (i one)", i=32))
-        nc.sync.dma_start(out=words[:].bitcast(I32), in_=k_words[0].rearrange("p t b -> p (t b)").bitcast(I32))
+        nc.sync.dma_start(out=words[:, T_HEAD:T].bitcast(I32), in_=words_hbm[:, T_HEAD:T])
         nc.sync.dma_start(out=q_raw[0][:], in_=q_rows(0))
         nc.sync.dma_start(out=q_raw[1][:], in_=q_rows(1))
-        nc.vector.memset(rows[32:64, :], 0)
-        nc.vector.memset(rows[64:128, :], 0)
         nc.vector.memset(planes[:], 0)
 
         log_pd = keep.tile([P, N], F32, name="log_pd")
@@ -76,7 +78,7 @@ def tile_attend_accept_srt_kernel(tc, qT, k_words, k_scales, ls, pd, offs, out):
         for quad in range(4):
             nc.sync.dma_start(
                 out=planes[32 * quad : 32 * quad + 4, :],
-                in_=picked_rows[8 * quad : 8 * quad + 8, :].bitcast(I32),
+                in_=picked_rows[32 * quad : 32 * quad + 32 : 4, :].bitcast(I32),
             )
         inv_pd = keep.tile([P, CHUNK], F32, name="inv_pd")
         nc.scalar.activation(out=inv_pd[:], in_=log_pd[:, 0:CHUNK], func=ACT.Exp, scale=-1.0)

@@ -112,18 +112,16 @@ def tile_attend_accept_srt_kernel(tc, qT, k_words, k_scales, ls, pd, offs, out):
                 stop=(o == PASSES - 1),
             )
 
-        head = codes_tile(0, 0, CHUNK, "k_head")
-        split(0, 0, CHUNK, head[:])
         quantize_q(0)
-        multiply(0, 0, head[:])
-        middle = codes_tile(0, CHUNK, N + CHUNK, "q_raw0")
-        split(0, CHUNK, 2 * CHUNK, middle[:, 0 : 2 * CHUNK])
-        split(0, 2 * CHUNK, N, middle[:, 2 * CHUNK : 2 * (N - CHUNK)])
-        for c in range(1, CHUNKS):
-            multiply(0, c, middle[:, 2 * (c - 1) * CHUNK : 2 * c * CHUNK])
-        split(1, 0, CHUNK, middle[:, 2 * (N - CHUNK) : 2 * N])
+        early = codes_tile(0, 0, N + CHUNK, "q_raw0")
+        split(0, 0, CHUNK, early[:, 0 : 2 * CHUNK])
+        split(0, CHUNK, 2 * CHUNK, early[:, 2 * CHUNK : 4 * CHUNK])
+        split(0, 2 * CHUNK, N, early[:, 4 * CHUNK : 2 * N])
+        for c in range(CHUNKS):
+            multiply(0, c, early[:, 2 * c * CHUNK : 2 * (c + 1) * CHUNK])
+        split(1, 0, CHUNK, early[:, 2 * N : 2 * (N + CHUNK)])
         quantize_q(1)
-        multiply(1, 0, middle[:, 2 * (N - CHUNK) : 2 * N])
+        multiply(1, 0, early[:, 2 * N : 2 * (N + CHUNK)])
         tail = codes_tile(1, CHUNK, N, "q_raw1")
         split(1, CHUNK, 2 * CHUNK, tail[:, 0 : 2 * CHUNK])
         split(1, 2 * CHUNK, N, tail[:, 2 * CHUNK : 2 * (N - CHUNK)])

@@ -22,50 +22,49 @@ K_PASS = P * PACK
 PASSES = D // K_PASS
 CHUNK = 128
 CHUNKS = N // CHUNK
-T_HEAD = T // 4
+SCALE_ROWS = D // 32
 
 
 def tile_attend_accept_srt_kernel(tc, qT, k_words, k_scales, ls, pd, offs, out):
     nc = tc.nc
     with ExitStack() as ctx:
         keep = ctx.enter_context(tc.tile_pool(name="keep", bufs=1))
+        reuse = ctx.enter_context(tc.tile_pool(name="reuse", bufs=1))
         psum = ctx.enter_context(tc.psum_pool(name="psum", bufs=1))
 
         offsets = keep.tile([P, N // 16], U16, name="offsets")
         words = keep.tile([P, T], U32, name="words")
         rows = keep.tile([P, T // 4], I32, name="rows")
         planes = keep.tile([P, PASSES * N // 4], I32, name="planes", align_bytes=64)
-        pd_sb = keep.tile([P, N], F32, name="pd_sb")
+        pd_sb = reuse.tile([P, N], F32, name="pd_sb", offset=256, align_bytes=64)
         ls_rows = keep.tile([P, 32], F32, name="ls_rows", align_bytes=64)
         q_raw = [keep.tile([P, PACK, NQ], F32, name="q_raw%d" % o, tag="q_raw%d" % o, align_bytes=64) for o in range(PASSES)]
 
         def q_rows(o):
             return qT[0, o * K_PASS : (o + 1) * K_PASS, :].rearrange("(p j) w -> p j w", j=PACK)
 
-        words_hbm = k_words[0].rearrange("p t b -> p (t b)").bitcast(I32)
-        nc.vector.memset(ls_rows[:], 0.0)
-        nc.vector.memset(rows[:], 0)
-        nc.scalar.dma_start(out=pd_sb[:], in_=pd[0])
-        nc.sync.dma_start(out=rows[0:P:4, :], in_=k_scales.bitcast(I32).rearrange("o f t -> f o t"))
-        nc.sync.dma_start(out=words[:, 0:T_HEAD].bitcast(I32), in_=words_hbm[:, 0:T_HEAD])
+        nc.scalar.dma_start(out=q_raw[0][:], in_=q_rows(0))
+        nc.sync.dma_start(out=rows[0:SCALE_ROWS, :], in_=k_scales.bitcast(I32).rearrange("o f t -> f o t"))
         nc.sync.dma_start(offsets[:], offs)
+        nc.vector.memset(ls_rows[:], 0.0)
         nc.sync.dma_start(out=ls_rows[0:P:32, :], in_=ls[0].rearrange("(g i) one -> g (i one)", i=32))
-        nc.sync.dma_start(out=words[:, T_HEAD:T].bitcast(I32), in_=words_hbm[:, T_HEAD:T])
-        nc.sync.dma_start(out=q_raw[0][:], in_=q_rows(0))
+        nc.sync.dma_start(out=words[:].bitcast(I32), in_=k_words[0].rearrange("p t b -> p (t b)").bitcast(I32))
+        nc.sync.dma_start(out=pd_sb[:], in_=pd[0])
         nc.sync.dma_start(out=q_raw[1][:], in_=q_rows(1))
+        nc.vector.memset(rows[32:64, :], 0)
+        nc.vector.memset(rows[64:P, :], 0)
         nc.vector.memset(planes[:], 0)
 
-        log_pd = keep.tile([P, N], F32, name="log_pd")
-        nc.scalar.activation(out=log_pd[:], in_=pd_sb[:], func=ACT.Ln)
-
-        q_bf = [keep.tile([P, NQ, PACK], BF16, name="q_bf%d" % o, tag="q_bf%d" % o, align_bytes=64) for o in range(PASSES)]
-        q_codes = [keep.tile([P, NQ], U32, name="q_codes%d" % o, align_bytes=64) for o in range(PASSES)]
+        q_bf = [keep.tile([P, NQ, PACK], BF16, name="q_bf%d" % o, align_bytes=64) for o in range(PASSES)]
+        q_codes = [
+            keep.tile([P, NQ], U32, name="q_codes0", align_bytes=64),
+            reuse.tile([P, NQ], U32, name="q_codes1", offset=PASSES * 2 * N, align_bytes=64),
+        ]
         q_scale = [keep.tile([P, NQ], U8, name="q_scale%d" % o, align_bytes=64) for o in range(PASSES)]
 
-        def round_q(o):
-            nc.scalar.copy(
-                out=q_bf[o][:].rearrange("p (c i) j -> p c j i", i=4),
-                in_=q_raw[o][:].rearrange("p j (c i) -> p c j i", i=4),
+        def round_q(o, first, last):
+            nc.vector.tensor_copy(
+                out=q_bf[o][:, first:last, :], in_=q_raw[o][:, :, first:last].rearrange("p j w -> p w j")
             )
 
         def quantize_q(o):
@@ -77,70 +76,72 @@ def tile_attend_accept_srt_kernel(tc, qT, k_words, k_scales, ls, pd, offs, out):
         nc.vector.tensor_copy(picked_rows[:], rows[:].bitcast(U8).indirect(offsets[:]))
         for quad in range(4):
             nc.sync.dma_start(
-                out=planes[32 * quad : 32 * quad + 4, :],
-                in_=picked_rows[32 * quad : 32 * quad + 32 : 4, :].bitcast(I32),
+                out=planes[32 * quad : 32 * quad + 4, :], in_=picked_rows[8 * quad : 8 * quad + 8, :].bitcast(I32)
             )
-        inv_pd = keep.tile([P, CHUNK], F32, name="inv_pd")
-        nc.scalar.activation(out=inv_pd[:], in_=log_pd[:, 0:CHUNK], func=ACT.Exp, scale=-1.0)
+        round_q(0, 0, NQ)
         neg_ls = keep.tile([P, 1], F32, name="neg_ls")
         ls_cols = keep.tile([P, 32], F32, name="ls_cols", align_bytes=64)
         nc.vector.transpose(out=ls_cols[:], in_=ls_rows[:])
+        quantize_q(0)
         nc.vector.tensor_scalar_mul(out=neg_ls[:], in0=ls_cols[:, 0:1], scalar1=-1.0)
-        round_q(0)
-        round_q(1)
 
-        picked_words = keep.tile([P, N], U32, name="picked_words")
+        log_pd = keep.tile([P, N], F32, name="log_pd")
+        nc.scalar.activation(out=log_pd[:], in_=pd_sb[:], func=ACT.Ln)
+
+        picked_words = keep.tile([P, N], U32, name="picked_words", tag="picked_slot")
         nc.vector.tensor_copy(picked_words[:], words[:].indirect(offsets[:]))
         halves = picked_words[:].bitcast(U16).rearrange("p (n o) -> p o n", o=PASSES)
 
         banks = [psum.tile([P, CHUNK], F32, name="bank%d" % c) for c in range(CHUNKS)]
+        k_both = reuse.tile([P, PASSES * 2 * N], U8, name="k_both", offset=0, align_bytes=64)
+        k_codes = [k_both[:, 2 * N * o : 2 * N * (o + 1)] for o in range(PASSES)]
 
-        def codes_tile(o, first, last, tag):
-            return keep.tile([P, 2 * (last - first)], U8, name="k_codes%d_%d" % (o, first), tag=tag, align_bytes=64)
+        def split(o, first, last):
+            nc.vector.tensor_copy(
+                out=k_codes[o][:, 2 * first * CHUNK : 2 * last * CHUNK].bitcast(U16),
+                in_=halves[:, o, first * CHUNK : last * CHUNK],
+            )
 
-        def split(o, first, last, codes):
-            nc.vector.tensor_copy(out=codes.bitcast(U16), in_=halves[:, o, first:last])
-
-        def multiply(o, c, codes):
+        def multiply(o, c):
             nc.tensor.matmul_mx(
                 out=banks[c][:],
                 lhsT=q_codes[o][:].bitcast(FP8X4),
                 lhsT_scale=q_scale[o][:],
-                rhs=codes.bitcast(FP4X4),
+                rhs=k_codes[o][:, 2 * c * CHUNK : 2 * (c + 1) * CHUNK].bitcast(FP4X4),
                 rhs_scale=planes[:].bitcast(U8)[:, o * N + c * CHUNK : o * N + (c + 1) * CHUNK],
                 start=(o == 0),
                 stop=(o == PASSES - 1),
             )
 
-        quantize_q(0)
-        early = codes_tile(0, 0, N + CHUNK, "q_raw0")
-        split(0, 0, CHUNK, early[:, 0 : 2 * CHUNK])
-        split(0, CHUNK, 2 * CHUNK, early[:, 2 * CHUNK : 4 * CHUNK])
-        split(0, 2 * CHUNK, N, early[:, 4 * CHUNK : 2 * N])
-        for c in range(CHUNKS):
-            multiply(0, c, early[:, 2 * c * CHUNK : 2 * (c + 1) * CHUNK])
-        split(1, 0, CHUNK, early[:, 2 * N : 2 * (N + CHUNK)])
+        last = CHUNKS - 1
+        round_q(1, 0, NQ)
+        for c in range(last):
+            split(0, c, c + 1)
         quantize_q(1)
-        multiply(1, 0, early[:, 2 * N : 2 * (N + CHUNK)])
-        tail = codes_tile(1, CHUNK, N, "q_raw1")
-        split(1, CHUNK, 2 * CHUNK, tail[:, 0 : 2 * CHUNK])
-        split(1, 2 * CHUNK, N, tail[:, 2 * CHUNK : 2 * (N - CHUNK)])
-        for c in range(1, CHUNKS):
-            multiply(1, c, tail[:, 2 * (c - 1) * CHUNK : 2 * c * CHUNK])
+        for c in range(last):
+            split(1, c, c + 1)
+        nc.vector.tensor_copy(
+            out=k_both[:].bitcast(U16).rearrange("p (o n) -> p o n", o=PASSES)[:, :, last * CHUNK : N],
+            in_=halves[:, :, last * CHUNK : N],
+        )
+        for o in range(PASSES):
+            for c in range(last):
+                multiply(o, c)
+        for o in range(PASSES):
+            multiply(o, last)
 
-        midway = [keep.tile([P, CHUNK], F32, name="midway%d" % c) for c in range(CHUNKS)]
+        log_ratio = keep.tile([P, N], F32, name="log_ratio", tag="picked_slot")
         ratio = [keep.tile([P, CHUNK], F32, name="ratio%d" % c) for c in range(CHUNKS)]
         result = [keep.tile([P, CHUNK], F32, name="result%d" % c) for c in range(CHUNKS)]
-        nc.scalar.activation(out=midway[0][:], in_=banks[0][:], func=ACT.Exp, bias=neg_ls[:])
-        for c in range(1, CHUNKS):
+        for c in range(CHUNKS):
+            cols = slice(c * CHUNK, (c + 1) * CHUNK)
             nc.vector.scalar_tensor_tensor(
-                out=midway[c][:], in0=banks[c][:], scalar=neg_ls[:], in1=log_pd[:, c * CHUNK : (c + 1) * CHUNK],
+                out=log_ratio[:, cols], in0=banks[c][:], scalar=neg_ls[:], in1=log_pd[:, cols],
                 op0=ALU.add, op1=ALU.subtract,
             )
-        nc.vector.tensor_tensor(out=ratio[0][:], in0=midway[0][:], in1=inv_pd[:], op=ALU.mult)
-        for c in range(1, CHUNKS):
-            nc.scalar.activation(out=ratio[c][:], in_=midway[c][:], func=ACT.Exp)
-        for c in (1, 0, 2, 3):
+        for c in range(CHUNKS):
+            nc.scalar.activation(out=ratio[c][:], in_=log_ratio[:, c * CHUNK : (c + 1) * CHUNK], func=ACT.Exp)
+        for c in range(CHUNKS):
             nc.vector.tensor_scalar_min(out=result[c][:], in0=ratio[c][:], scalar1=1.0)
             queue = nc.scalar if c == CHUNKS - 1 else nc.sync
             queue.dma_start(out=out[0, :, c * CHUNK : (c + 1) * CHUNK], in_=result[c][:])

@@ -115,11 +115,11 @@ def tile_attend_accept_srt_kernel(tc, qT, k_words, k_scales, ls, pd, offs, out):
 
         last = CHUNKS - 1
         round_q(1, 0, NQ)
-        for c in range(last):
-            split(0, c, c + 1)
+        split(0, 0, 1)
+        split(0, 1, last)
         quantize_q(1)
-        for c in range(last):
-            split(1, c, c + 1)
+        split(1, 0, 1)
+        split(1, 1, last)
         nc.vector.tensor_copy(
             out=k_both[:].bitcast(U16).rearrange("p (o n) -> p o n", o=PASSES)[:, :, last * CHUNK : N],
             in_=halves[:, :, last * CHUNK : N],
@@ -131,17 +131,20 @@ def tile_attend_accept_srt_kernel(tc, qT, k_words, k_scales, ls, pd, offs, out):
             multiply(o, last)
 
         log_ratio = keep.tile([P, N], F32, name="log_ratio", tag="picked_slot")
-        ratio = [keep.tile([P, CHUNK], F32, name="ratio%d" % c) for c in range(CHUNKS)]
+        ratio = keep.tile([P, N], F32, name="ratio")
         result = [keep.tile([P, CHUNK], F32, name="result%d" % c) for c in range(CHUNKS)]
-        for c in range(CHUNKS):
-            cols = slice(c * CHUNK, (c + 1) * CHUNK)
+        pieces = [(c, 0, CHUNK) for c in range(last)] + [(last, 0, CHUNK // 2), (last, CHUNK // 2, CHUNK)]
+        for c, a, b in pieces:
+            cols = slice(c * CHUNK + a, c * CHUNK + b)
             nc.vector.scalar_tensor_tensor(
-                out=log_ratio[:, cols], in0=banks[c][:], scalar=neg_ls[:], in1=log_pd[:, cols],
+                out=log_ratio[:, cols], in0=banks[c][:, a:b], scalar=neg_ls[:], in1=log_pd[:, cols],
                 op0=ALU.add, op1=ALU.subtract,
             )
-        for c in range(CHUNKS):
-            nc.scalar.activation(out=ratio[c][:], in_=log_ratio[:, c * CHUNK : (c + 1) * CHUNK], func=ACT.Exp)
-        for c in range(CHUNKS):
-            nc.vector.tensor_scalar_min(out=result[c][:], in0=ratio[c][:], scalar1=1.0)
-            queue = nc.scalar if c == CHUNKS - 1 else nc.sync
-            queue.dma_start(out=out[0, :, c * CHUNK : (c + 1) * CHUNK], in_=result[c][:])
+        for c, a, b in pieces:
+            cols = slice(c * CHUNK + a, c * CHUNK + b)
+            nc.scalar.activation(out=ratio[:, cols], in_=log_ratio[:, cols], func=ACT.Exp)
+        for c, a, b in pieces:
+            nc.vector.tensor_scalar_min(out=result[c][:, a:b], in0=ratio[:, c * CHUNK + a : c * CHUNK + b], scalar1=1.0)
+            if b == CHUNK:
+                queue = nc.scalar if c == last else nc.sync
+                queue.dma_start(out=out[0, :, c * CHUNK : (c + 1) * CHUNK], in_=result[c][:])

@@ -23,6 +23,7 @@ PASSES = D // K_PASS
 CHUNK = 128
 CHUNKS = N // CHUNK
 SCALE_ROWS = D // 32
+Q_VECTOR = 64
 
 
 def tile_attend_accept_srt_kernel(tc, qT, k_words, k_scales, ls, pd, offs, out):
@@ -58,7 +59,7 @@ def tile_attend_accept_srt_kernel(tc, qT, k_words, k_scales, ls, pd, offs, out):
         q_bf = [keep.tile([P, NQ, PACK], BF16, name="q_bf%d" % o, align_bytes=64) for o in range(PASSES)]
         q_codes = [
             keep.tile([P, NQ], U32, name="q_codes0", align_bytes=64),
-            reuse.tile([P, NQ], U32, name="q_codes1", offset=PASSES * 2 * N, align_bytes=64),
+            keep.tile([P, NQ], U32, name="q_codes1", align_bytes=64),
         ]
         q_scale = [keep.tile([P, NQ], U8, name="q_scale%d" % o, align_bytes=64) for o in range(PASSES)]
 
@@ -93,35 +94,41 @@ def tile_attend_accept_srt_kernel(tc, qT, k_words, k_scales, ls, pd, offs, out):
         halves = picked_words[:].bitcast(U16).rearrange("p (n o) -> p o n", o=PASSES)
 
         banks = [psum.tile([P, CHUNK], F32, name="bank%d" % c) for c in range(CHUNKS)]
-        k_both = reuse.tile([P, PASSES * 2 * N], U8, name="k_both", offset=0, align_bytes=64)
-        k_codes = [k_both[:, 2 * N * o : 2 * N * (o + 1)] for o in range(PASSES)]
+        last = CHUNKS - 1
+        early = reuse.tile([P, 2 * last * CHUNK], U8, name="k_early", offset=0, align_bytes=64)
+        late = keep.tile([P, 2 * (last + PASSES) * CHUNK], U8, name="k_late", tag="q_raw1", align_bytes=64)
 
-        def split(o, first, last):
-            nc.vector.tensor_copy(
-                out=k_codes[o][:, 2 * first * CHUNK : 2 * last * CHUNK].bitcast(U16),
-                in_=halves[:, o, first * CHUNK : last * CHUNK],
-            )
+        def codes(o, first, end):
+            if first == last:
+                return late[:, 2 * (last + o) * CHUNK : 2 * (last + o + 1) * CHUNK]
+            return (early, late)[o][:, 2 * first * CHUNK : 2 * end * CHUNK]
+
+        def split(o, first, end):
+            nc.vector.tensor_copy(out=codes(o, first, end).bitcast(U16), in_=halves[:, o, first * CHUNK : end * CHUNK])
 
         def multiply(o, c):
             nc.tensor.matmul_mx(
                 out=banks[c][:],
                 lhsT=q_codes[o][:].bitcast(FP8X4),
                 lhsT_scale=q_scale[o][:],
-                rhs=k_codes[o][:, 2 * c * CHUNK : 2 * (c + 1) * CHUNK].bitcast(FP4X4),
+                rhs=codes(o, c, c + 1).bitcast(FP4X4),
                 rhs_scale=planes[:].bitcast(U8)[:, o * N + c * CHUNK : o * N + (c + 1) * CHUNK],
                 start=(o == 0),
                 stop=(o == PASSES - 1),
             )
 
-        last = CHUNKS - 1
-        round_q(1, 0, NQ)
+        round_q(1, 0, Q_VECTOR)
+        nc.scalar.copy(
+            out=q_bf[1][:, Q_VECTOR:NQ, :].rearrange("p (c i) j -> p c j i", i=4),
+            in_=q_raw[1][:, :, Q_VECTOR:NQ].rearrange("p j (c i) -> p c j i", i=4),
+        )
         split(0, 0, 1)
         split(0, 1, last)
         quantize_q(1)
         split(1, 0, 1)
         split(1, 1, last)
         nc.vector.tensor_copy(
-            out=k_both[:].bitcast(U16).rearrange("p (o n) -> p o n", o=PASSES)[:, :, last * CHUNK : N],
+            out=late[:, 2 * last * CHUNK :].bitcast(U16).rearrange("p (o n) -> p o n", o=PASSES),
             in_=halves[:, :, last * CHUNK : N],
         )
         for o in range(PASSES):

@@ -95,23 +95,27 @@ def tile_attend_accept_srt_kernel(tc, qT, k_words, k_scales, ls, pd, offs, out):
 
         banks = [psum.tile([P, CHUNK], F32, name="bank%d" % c) for c in range(CHUNKS)]
         last = CHUNKS - 1
-        early = reuse.tile([P, 2 * last * CHUNK], U8, name="k_early", offset=0, align_bytes=64)
-        late = keep.tile([P, 2 * (last + PASSES) * CHUNK], U8, name="k_late", tag="q_raw1", align_bytes=64)
+        early_parts = [(0, c) for c in range(CHUNKS)]
+        late_parts = [(1, c) for c in range(CHUNKS)]
+        early = reuse.tile([P, 2 * len(early_parts) * CHUNK], U8, name="k_early", offset=0, align_bytes=64)
+        late = keep.tile([P, 2 * len(late_parts) * CHUNK], U8, name="k_late", tag="q_raw1", align_bytes=64)
 
-        def codes(o, first, end):
-            if first == last:
-                return late[:, 2 * (last + o) * CHUNK : 2 * (last + o + 1) * CHUNK]
-            return (early, late)[o][:, 2 * first * CHUNK : 2 * end * CHUNK]
+        def codes(o, c, count=1):
+            tile, parts = (early, early_parts) if (o, c) in early_parts else (late, late_parts)
+            at = parts.index((o, c))
+            return tile[:, 2 * at * CHUNK : 2 * (at + count) * CHUNK]
 
         def split(o, first, end):
-            nc.vector.tensor_copy(out=codes(o, first, end).bitcast(U16), in_=halves[:, o, first * CHUNK : end * CHUNK])
+            nc.vector.tensor_copy(
+                out=codes(o, first, end - first).bitcast(U16), in_=halves[:, o, first * CHUNK : end * CHUNK]
+            )
 
         def multiply(o, c):
             nc.tensor.matmul_mx(
                 out=banks[c][:],
                 lhsT=q_codes[o][:].bitcast(FP8X4),
                 lhsT_scale=q_scale[o][:],
-                rhs=codes(o, c, c + 1).bitcast(FP4X4),
+                rhs=codes(o, c).bitcast(FP4X4),
                 rhs_scale=planes[:].bitcast(U8)[:, o * N + c * CHUNK : o * N + (c + 1) * CHUNK],
                 start=(o == 0),
                 stop=(o == PASSES - 1),
@@ -123,23 +127,19 @@ def tile_attend_accept_srt_kernel(tc, qT, k_words, k_scales, ls, pd, offs, out):
             in_=q_raw[1][:, :, Q_VECTOR:NQ].rearrange("p j (c i) -> p c j i", i=4),
         )
         split(0, 0, 1)
-        split(0, 1, last)
+        split(0, 1, 2)
+        split(0, 2, CHUNKS)
         quantize_q(1)
         split(1, 0, 1)
-        split(1, 1, last)
-        nc.vector.tensor_copy(
-            out=late[:, 2 * last * CHUNK :].bitcast(U16).rearrange("p (o n) -> p o n", o=PASSES),
-            in_=halves[:, :, last * CHUNK : N],
-        )
+        split(1, 1, 2)
+        split(1, 2, CHUNKS)
         for o in range(PASSES):
-            for c in range(last):
+            for c in range(CHUNKS):
                 multiply(o, c)
-        for o in range(PASSES):
-            multiply(o, last)
 
         log_ratio = keep.tile([P, N], F32, name="log_ratio", tag="picked_slot")
         ratio = keep.tile([P, N], F32, name="ratio")
-        result = [keep.tile([P, CHUNK], F32, name="result%d" % c) for c in range(CHUNKS)]
+        result = [keep.tile([P, 2 * CHUNK], F32, name="result%d" % pair) for pair in range(CHUNKS // 2)]
         pieces = [(c, 0, CHUNK) for c in range(last)] + [(last, 0, CHUNK // 2), (last, CHUNK // 2, CHUNK)]
         for c, a, b in pieces:
             cols = slice(c * CHUNK + a, c * CHUNK + b)
@@ -151,7 +151,7 @@ def tile_attend_accept_srt_kernel(tc, qT, k_words, k_scales, ls, pd, offs, out):
             cols = slice(c * CHUNK + a, c * CHUNK + b)
             nc.scalar.activation(out=ratio[:, cols], in_=log_ratio[:, cols], func=ACT.Exp)
         for c, a, b in pieces:
-            nc.vector.tensor_scalar_min(out=result[c][:, a:b], in0=ratio[:, c * CHUNK + a : c * CHUNK + b], scalar1=1.0)
-            if b == CHUNK:
+            nc.vector.tensor_scalar_min(out=result[c // 2][:, c % 2 * CHUNK + a : c % 2 * CHUNK + b], in0=ratio[:, c * CHUNK + a : c * CHUNK + b], scalar1=1.0)
+            if b == CHUNK and c % 2 == 1:
                 queue = nc.scalar if c == last else nc.sync
-                queue.dma_start(out=out[0, :, c * CHUNK : (c + 1) * CHUNK], in_=result[c][:])
+                queue.dma_start(out=out[0, :, (c - 1) * CHUNK : (c + 1) * CHUNK], in_=result[c // 2][:])

@@ -20,6 +20,7 @@ P = 128
 PACK = 4
 K_PASS = P * PACK
 PASSES = D // K_PASS
+HALF = N // 2
 CHUNK = 128
 CHUNKS = N // CHUNK
 SCALE_ROWS = D // 32
@@ -37,7 +38,7 @@ def tile_attend_accept_srt_kernel(tc, qT, k_words, k_scales, ls, pd, offs, out):
         words = keep.tile([P, T], U32, name="words")
         rows = keep.tile([P, T // 4], I32, name="rows")
         planes = keep.tile([P, PASSES * N // 4], I32, name="planes", align_bytes=64)
-        pd_sb = reuse.tile([P, N], F32, name="pd_sb", offset=256, align_bytes=64)
+        pd_sb = reuse.tile([P, N], F32, name="pd_sb", offset=0, align_bytes=64)
         ls_rows = keep.tile([P, 32], F32, name="ls_rows", align_bytes=64)
         q_raw = [keep.tile([P, PACK, NQ], F32, name="q_raw%d" % o, tag="q_raw%d" % o, align_bytes=64) for o in range(PASSES)]
 
@@ -57,10 +58,7 @@ def tile_attend_accept_srt_kernel(tc, qT, k_words, k_scales, ls, pd, offs, out):
         nc.vector.memset(planes[:], 0)
 
         q_bf = [keep.tile([P, NQ, PACK], BF16, name="q_bf%d" % o, align_bytes=64) for o in range(PASSES)]
-        q_codes = [
-            keep.tile([P, NQ], U32, name="q_codes0", align_bytes=64),
-            keep.tile([P, NQ], U32, name="q_codes1", align_bytes=64),
-        ]
+        q_codes = [keep.tile([P, NQ], U32, name="q_codes%d" % o, align_bytes=64) for o in range(PASSES)]
         q_scale = [keep.tile([P, NQ], U8, name="q_scale%d" % o, align_bytes=64) for o in range(PASSES)]
 
         def round_q(o, first, last):
@@ -80,34 +78,34 @@ def tile_attend_accept_srt_kernel(tc, qT, k_words, k_scales, ls, pd, offs, out):
                 out=planes[32 * quad : 32 * quad + 4, :], in_=picked_rows[8 * quad : 8 * quad + 8, :].bitcast(I32)
             )
         round_q(0, 0, NQ)
-        neg_ls = keep.tile([P, 1], F32, name="neg_ls")
         ls_cols = keep.tile([P, 32], F32, name="ls_cols", align_bytes=64)
         nc.vector.transpose(out=ls_cols[:], in_=ls_rows[:])
         quantize_q(0)
-        nc.vector.tensor_scalar_mul(out=neg_ls[:], in0=ls_cols[:, 0:1], scalar1=-1.0)
 
         log_pd = keep.tile([P, N], F32, name="log_pd")
         nc.scalar.activation(out=log_pd[:], in_=pd_sb[:], func=ACT.Ln)
 
-        picked_words = keep.tile([P, N], U32, name="picked_words", tag="picked_slot")
-        nc.vector.tensor_copy(picked_words[:], words[:].indirect(offsets[:]))
-        halves = picked_words[:].bitcast(U16).rearrange("p (n o) -> p o n", o=PASSES)
+        picked = [keep.tile([P, HALF], U32, name="picked%d" % h) for h in range(2)]
+        for h in range(2):
+            nc.vector.tensor_copy(picked[h][:], words[:].indirect(offsets[:, h * HALF // 16 : (h + 1) * HALF // 16]))
 
         banks = [psum.tile([P, CHUNK], F32, name="bank%d" % c) for c in range(CHUNKS)]
-        last = CHUNKS - 1
-        early_parts = [(0, c) for c in range(CHUNKS)]
-        late_parts = [(1, c) for c in range(CHUNKS)]
-        early = reuse.tile([P, 2 * len(early_parts) * CHUNK], U8, name="k_early", offset=0, align_bytes=64)
-        late = keep.tile([P, 2 * len(late_parts) * CHUNK], U8, name="k_late", tag="q_raw1", align_bytes=64)
+        first_codes = keep.tile([P, 2 * CHUNK], U8, name="k_first", align_bytes=64)
+        early = reuse.tile([P, 2 * CHUNKS * CHUNK], U8, name="k_early", offset=0, align_bytes=64)
+        late = keep.tile([P, 2 * (CHUNKS - 1) * CHUNK], U8, name="k_late", tag="q_raw1", align_bytes=64)
 
         def codes(o, c, count=1):
-            tile, parts = (early, early_parts) if (o, c) in early_parts else (late, late_parts)
-            at = parts.index((o, c))
+            step = o * CHUNKS + c
+            if step == 0:
+                return first_codes[:]
+            tile, at = (early, step - 1) if step <= CHUNKS else (late, step - CHUNKS - 1)
             return tile[:, 2 * at * CHUNK : 2 * (at + count) * CHUNK]
 
         def split(o, first, end):
+            h, at = divmod(first * CHUNK, HALF)
+            pairs = picked[h][:].bitcast(U16).rearrange("p (n o) -> p o n", o=PASSES)
             nc.vector.tensor_copy(
-                out=codes(o, first, end - first).bitcast(U16), in_=halves[:, o, first * CHUNK : end * CHUNK]
+                out=codes(o, first, end - first).bitcast(U16), in_=pairs[:, o, at : at + (end - first) * CHUNK]
             )
 
         def multiply(o, c):
@@ -121,37 +119,41 @@ def tile_attend_accept_srt_kernel(tc, qT, k_words, k_scales, ls, pd, offs, out):
                 stop=(o == PASSES - 1),
             )
 
+        split(0, 0, 1)
         round_q(1, 0, Q_VECTOR)
         nc.scalar.copy(
             out=q_bf[1][:, Q_VECTOR:NQ, :].rearrange("p (c i) j -> p c j i", i=4),
             in_=q_raw[1][:, :, Q_VECTOR:NQ].rearrange("p j (c i) -> p c j i", i=4),
         )
-        split(0, 0, 1)
         split(0, 1, 2)
         split(0, 2, CHUNKS)
-        quantize_q(1)
         split(1, 0, 1)
+        quantize_q(1)
         split(1, 1, 2)
         split(1, 2, CHUNKS)
         for o in range(PASSES):
             for c in range(CHUNKS):
                 multiply(o, c)
 
-        log_ratio = keep.tile([P, N], F32, name="log_ratio", tag="picked_slot")
+        log_ratio = keep.tile([P, N], F32, name="log_ratio")
         ratio = keep.tile([P, N], F32, name="ratio")
-        result = [keep.tile([P, 2 * CHUNK], F32, name="result%d" % pair) for pair in range(CHUNKS // 2)]
+        result = [keep.tile([P, HALF], F32, name="result%d" % h) for h in range(2)]
+        last = CHUNKS - 1
         pieces = [(c, 0, CHUNK) for c in range(last)] + [(last, 0, CHUNK // 2), (last, CHUNK // 2, CHUNK)]
         for c, a, b in pieces:
             cols = slice(c * CHUNK + a, c * CHUNK + b)
             nc.vector.scalar_tensor_tensor(
-                out=log_ratio[:, cols], in0=banks[c][:, a:b], scalar=neg_ls[:], in1=log_pd[:, cols],
-                op0=ALU.add, op1=ALU.subtract,
+                out=log_ratio[:, cols], in0=banks[c][:, a:b], scalar=ls_cols[:, 0:1], in1=log_pd[:, cols],
+                op0=ALU.subtract, op1=ALU.subtract,
             )
         for c, a, b in pieces:
             cols = slice(c * CHUNK + a, c * CHUNK + b)
             nc.scalar.activation(out=ratio[:, cols], in_=log_ratio[:, cols], func=ACT.Exp)
         for c, a, b in pieces:
-            nc.vector.tensor_scalar_min(out=result[c // 2][:, c % 2 * CHUNK + a : c % 2 * CHUNK + b], in0=ratio[:, c * CHUNK + a : c * CHUNK + b], scalar1=1.0)
+            at = c % 2 * CHUNK
+            nc.vector.tensor_scalar_min(
+                out=result[c // 2][:, at + a : at + b], in0=ratio[:, c * CHUNK + a : c * CHUNK + b], scalar1=1.0
+            )
             if b == CHUNK and c % 2 == 1:
                 queue = nc.scalar if c == last else nc.sync
                 queue.dma_start(out=out[0, :, (c - 1) * CHUNK : (c + 1) * CHUNK], in_=result[c // 2][:])

@@ -24,7 +24,6 @@ HALF = N // 2
 CHUNK = 128
 CHUNKS = N // CHUNK
 SCALE_ROWS = D // 32
-Q_VECTOR = 64
 
 
 def tile_attend_accept_srt_kernel(tc, qT, k_words, k_scales, ls, pd, offs, out):
@@ -59,16 +58,21 @@ def tile_attend_accept_srt_kernel(tc, qT, k_words, k_scales, ls, pd, offs, out):
 
         q_bf = [keep.tile([P, NQ, PACK], BF16, name="q_bf%d" % o, align_bytes=64) for o in range(PASSES)]
         q_codes = [keep.tile([P, NQ], U32, name="q_codes%d" % o, align_bytes=64) for o in range(PASSES)]
-        q_scale = [keep.tile([P, NQ], U8, name="q_scale%d" % o, align_bytes=64) for o in range(PASSES)]
+        q_scale = [
+            keep.tile([P, NQ], U8, name="q_scale0", align_bytes=64),
+            reuse.tile([P, NQ], U8, name="q_scale1", offset=2 * N, align_bytes=64),
+        ]
 
         def round_q(o, first, last):
             nc.vector.tensor_copy(
                 out=q_bf[o][:, first:last, :], in_=q_raw[o][:, :, first:last].rearrange("p j w -> p w j")
             )
 
-        def quantize_q(o):
+        def quantize_q(o, first, last):
             nc.vector.quantize_mx(
-                out=q_codes[o][:].bitcast(FP8X4), scales=q_scale[o][:], in_=q_bf[o][:].rearrange("p w j -> p (w j)")
+                out=q_codes[o][:, first:last].bitcast(FP8X4),
+                scales=q_scale[o][:, first:last],
+                in_=q_bf[o][:, first:last, :].rearrange("p w j -> p (w j)"),
             )
 
         picked_rows = keep.tile([P, N], U8, name="picked_rows")
@@ -80,7 +84,7 @@ def tile_attend_accept_srt_kernel(tc, qT, k_words, k_scales, ls, pd, offs, out):
         round_q(0, 0, NQ)
         ls_cols = keep.tile([P, 32], F32, name="ls_cols", align_bytes=64)
         nc.vector.transpose(out=ls_cols[:], in_=ls_rows[:])
-        quantize_q(0)
+        quantize_q(0, 0, NQ)
 
         log_pd = keep.tile([P, N], F32, name="log_pd")
         nc.scalar.activation(out=log_pd[:], in_=pd_sb[:], func=ACT.Ln)
@@ -90,16 +94,13 @@ def tile_attend_accept_srt_kernel(tc, qT, k_words, k_scales, ls, pd, offs, out):
             nc.vector.tensor_copy(picked[h][:], words[:].indirect(offsets[:, h * HALF // 16 : (h + 1) * HALF // 16]))
 
         banks = [psum.tile([P, CHUNK], F32, name="bank%d" % c) for c in range(CHUNKS)]
-        first_codes = keep.tile([P, 2 * CHUNK], U8, name="k_first", align_bytes=64)
-        early = reuse.tile([P, 2 * CHUNKS * CHUNK], U8, name="k_early", offset=0, align_bytes=64)
-        late = keep.tile([P, 2 * (CHUNKS - 1) * CHUNK], U8, name="k_late", tag="q_raw1", align_bytes=64)
+        parted = [
+            keep.tile([P, 2 * N], U8, name="parted0", align_bytes=64),
+            reuse.tile([P, 2 * N], U8, name="parted1", offset=0, align_bytes=64),
+        ]
 
         def codes(o, c, count=1):
-            step = o * CHUNKS + c
-            if step == 0:
-                return first_codes[:]
-            tile, at = (early, step - 1) if step <= CHUNKS else (late, step - CHUNKS - 1)
-            return tile[:, 2 * at * CHUNK : 2 * (at + count) * CHUNK]
+            return parted[o][:, 2 * c * CHUNK : 2 * (c + count) * CHUNK]
 
         def split(o, first, end):
             h, at = divmod(first * CHUNK, HALF)
@@ -120,16 +121,13 @@ def tile_attend_accept_srt_kernel(tc, qT, k_words, k_scales, ls, pd, offs, out):
             )
 
         split(0, 0, 1)
-        round_q(1, 0, Q_VECTOR)
-        nc.scalar.copy(
-            out=q_bf[1][:, Q_VECTOR:NQ, :].rearrange("p (c i) j -> p c j i", i=4),
-            in_=q_raw[1][:, :, Q_VECTOR:NQ].rearrange("p j (c i) -> p c j i", i=4),
-        )
         split(0, 1, 2)
         split(0, 2, CHUNKS)
-        split(1, 0, 1)
-        quantize_q(1)
-        split(1, 1, 2)
+        round_q(1, 0, NQ // 2)
+        round_q(1, NQ // 2, NQ)
+        split(1, 0, 2)
+        quantize_q(1, 0, NQ // 2)
+        quantize_q(1, NQ // 2, NQ)
         split(1, 2, CHUNKS)
         for o in range(PASSES):
             for c in range(CHUNKS):

@@ -24,6 +24,7 @@ HALF = N // 2
 CHUNK = 128
 CHUNKS = N // CHUNK
 SCALE_ROWS = D // 32
+Q_VECTOR = 96
 
 
 def tile_attend_accept_srt_kernel(tc, qT, k_words, k_scales, ls, pd, offs, out):
@@ -65,7 +66,8 @@ def tile_attend_accept_srt_kernel(tc, qT, k_words, k_scales, ls, pd, offs, out):
 
         def round_q(o, first, last):
             nc.vector.tensor_copy(
-                out=q_bf[o][:, first:last, :], in_=q_raw[o][:, :, first:last].rearrange("p j w -> p w j")
+                out=q_bf[o][:, first:last, :].rearrange("p (c i) j -> p c j i", i=4),
+                in_=q_raw[o][:, :, first:last].rearrange("p j (c i) -> p c j i", i=4),
             )
 
         def quantize_q(o, first, last):
@@ -94,13 +96,14 @@ def tile_attend_accept_srt_kernel(tc, qT, k_words, k_scales, ls, pd, offs, out):
             nc.vector.tensor_copy(picked[h][:], words[:].indirect(offsets[:, h * HALF // 16 : (h + 1) * HALF // 16]))
 
         banks = [psum.tile([P, CHUNK], F32, name="bank%d" % c) for c in range(CHUNKS)]
-        parted = [
-            keep.tile([P, 2 * N], U8, name="parted0", align_bytes=64),
-            reuse.tile([P, 2 * N], U8, name="parted1", offset=0, align_bytes=64),
-        ]
+        first_codes = keep.tile([P, 2 * HALF], U8, name="k_first", align_bytes=64)
+        early = reuse.tile([P, 2 * (HALF + CHUNK)], U8, name="k_early", offset=0, align_bytes=64)
+        late = keep.tile([P, 2 * (CHUNKS - 1) * CHUNK], U8, name="k_late", tag="q_raw1", align_bytes=64)
 
         def codes(o, c, count=1):
-            return parted[o][:, 2 * c * CHUNK : 2 * (c + count) * CHUNK]
+            step = o * CHUNKS + c
+            tile, at = (first_codes, step) if step < 2 else (early, step - 2) if step <= CHUNKS else (late, step - CHUNKS - 1)
+            return tile[:, 2 * at * CHUNK : 2 * (at + count) * CHUNK]
 
         def split(o, first, end):
             h, at = divmod(first * CHUNK, HALF)
@@ -122,12 +125,17 @@ def tile_attend_accept_srt_kernel(tc, qT, k_words, k_scales, ls, pd, offs, out):
 
         split(0, 0, 1)
         split(0, 1, 2)
-        split(0, 2, CHUNKS)
         round_q(1, 0, NQ // 2)
-        round_q(1, NQ // 2, NQ)
-        split(1, 0, 2)
+        round_q(1, NQ // 2, Q_VECTOR)
+        nc.scalar.copy(
+            out=q_bf[1][:, Q_VECTOR:NQ, :].rearrange("p (c i) j -> p c j i", i=4),
+            in_=q_raw[1][:, :, Q_VECTOR:NQ].rearrange("p j (c i) -> p c j i", i=4),
+        )
+        split(0, 2, CHUNKS)
+        split(1, 0, 1)
         quantize_q(1, 0, NQ // 2)
         quantize_q(1, NQ // 2, NQ)
+        split(1, 1, 2)
         split(1, 2, CHUNKS)
         for o in range(PASSES):
             for c in range(CHUNKS):

@@ -25,6 +25,7 @@ CHUNK = 128
 CHUNKS = N // CHUNK
 SCALE_ROWS = D // 32
 Q_VECTOR = 96
+DMA_ALIGN = 256
 
 
 def tile_attend_accept_srt_kernel(tc, qT, k_words, k_scales, ls, pd, offs, out):
@@ -35,12 +36,12 @@ def tile_attend_accept_srt_kernel(tc, qT, k_words, k_scales, ls, pd, offs, out):
         psum = ctx.enter_context(tc.psum_pool(name="psum", bufs=1))
 
         offsets = keep.tile([P, N // 16], U16, name="offsets")
-        words = keep.tile([P, T], U32, name="words")
-        rows = keep.tile([P, T // 4], I32, name="rows")
-        planes = keep.tile([P, PASSES * N // 4], I32, name="planes", align_bytes=64)
-        pd_sb = reuse.tile([P, N], F32, name="pd_sb", offset=0, align_bytes=64)
-        ls_rows = keep.tile([P, 32], F32, name="ls_rows", align_bytes=64)
-        q_raw = [keep.tile([P, PACK, NQ], F32, name="q_raw%d" % o, tag="q_raw%d" % o, align_bytes=64) for o in range(PASSES)]
+        words = keep.tile([P, T], U32, name="words", align_bytes=DMA_ALIGN)
+        rows = keep.tile([P, T // 4], I32, name="rows", align_bytes=DMA_ALIGN)
+        planes = keep.tile([P, PASSES * N // 4], I32, name="planes", align_bytes=DMA_ALIGN)
+        pd_sb = reuse.tile([P, N], F32, name="pd_sb", offset=0, align_bytes=DMA_ALIGN)
+        ls_rows = keep.tile([P, 32], F32, name="ls_rows", align_bytes=DMA_ALIGN)
+        q_raw = [keep.tile([P, PACK, NQ], F32, name="q_raw%d" % o, tag="q_raw%d" % o, align_bytes=DMA_ALIGN) for o in range(PASSES)]
 
         def q_rows(o):
             return qT[0, o * K_PASS : (o + 1) * K_PASS, :].rearrange("(p j) w -> p j w", j=PACK)
@@ -77,7 +78,7 @@ def tile_attend_accept_srt_kernel(tc, qT, k_words, k_scales, ls, pd, offs, out):
                 in_=q_bf[o][:, first:last, :].rearrange("p w j -> p (w j)"),
             )
 
-        picked_rows = keep.tile([P, N], U8, name="picked_rows")
+        picked_rows = keep.tile([P, N], U8, name="picked_rows", align_bytes=DMA_ALIGN)
         nc.vector.tensor_copy(picked_rows[:], rows[:].bitcast(U8).indirect(offsets[:]))
         for quad in range(4):
             nc.sync.dma_start(
@@ -98,7 +99,7 @@ def tile_attend_accept_srt_kernel(tc, qT, k_words, k_scales, ls, pd, offs, out):
         banks = [psum.tile([P, CHUNK], F32, name="bank%d" % c) for c in range(CHUNKS)]
         first_codes = keep.tile([P, 2 * HALF], U8, name="k_first", align_bytes=64)
         early = reuse.tile([P, 2 * (HALF + CHUNK)], U8, name="k_early", offset=0, align_bytes=64)
-        late = keep.tile([P, 2 * (CHUNKS - 1) * CHUNK], U8, name="k_late", tag="q_raw1", align_bytes=64)
+        late = keep.tile([P, 2 * (CHUNKS - 1) * CHUNK], U8, name="k_late", tag="q_raw1", align_bytes=DMA_ALIGN)
 
         def codes(o, c, count=1):
             step = o * CHUNKS + c
@@ -143,7 +144,7 @@ def tile_attend_accept_srt_kernel(tc, qT, k_words, k_scales, ls, pd, offs, out):
 
         log_ratio = keep.tile([P, N], F32, name="log_ratio")
         ratio = keep.tile([P, N], F32, name="ratio")
-        result = [keep.tile([P, HALF], F32, name="result%d" % h) for h in range(2)]
+        result = [keep.tile([P, HALF], F32, name="result%d" % h, align_bytes=DMA_ALIGN) for h in range(2)]
         last = CHUNKS - 1
         pieces = [(c, 0, CHUNK) for c in range(last)] + [(last, 0, CHUNK // 2), (last, CHUNK // 2, CHUNK)]
         for c, a, b in pieces:

from contextlib import ExitStack

import concourse.mybir as mybir

D, T, N, NQ = 1024, 4096, 512, 128
FLOPS = 2 * NQ * N * D

F32 = mybir.dt.float32
BF16 = mybir.dt.bfloat16
I32 = mybir.dt.int32
U32 = mybir.dt.uint32
U16 = mybir.dt.uint16
U8 = mybir.dt.uint8
FP8X4 = mybir.dt.float8_e4m3fn_x4
FP4X4 = mybir.dt.float4_e2m1fn_x4
ALU = mybir.AluOpType
ACT = mybir.ActivationFunctionType

P = 128
PACK = 4
K_PASS = P * PACK
PASSES = D // K_PASS
HALF = N // 2
CHUNK = 128
CHUNKS = N // CHUNK
SCALE_ROWS = D // 32
Q_VECTOR = 96
DMA_ALIGN = 256


def tile_attend_accept_srt_kernel(tc, qT, k_words, k_scales, ls, pd, offs, out):
    nc = tc.nc
    with ExitStack() as ctx:
        keep = ctx.enter_context(tc.tile_pool(name="keep", bufs=1))
        reuse = ctx.enter_context(tc.tile_pool(name="reuse", bufs=1))
        psum = ctx.enter_context(tc.psum_pool(name="psum", bufs=1))

        offsets = keep.tile([P, N // 16], U16, name="offsets")
        words = keep.tile([P, T], U32, name="words", align_bytes=DMA_ALIGN)
        rows = keep.tile([P, T // 4], I32, name="rows", align_bytes=DMA_ALIGN)
        planes = keep.tile([P, PASSES * N // 4], I32, name="planes", align_bytes=DMA_ALIGN)
        pd_sb = reuse.tile([P, N], F32, name="pd_sb", offset=0, align_bytes=DMA_ALIGN)
        ls_rows = keep.tile([P, 32], F32, name="ls_rows", align_bytes=DMA_ALIGN)
        q_raw = [keep.tile([P, PACK, NQ], F32, name="q_raw%d" % o, tag="q_raw%d" % o, align_bytes=DMA_ALIGN) for o in range(PASSES)]

        def q_rows(o):
            return qT[0, o * K_PASS : (o + 1) * K_PASS, :].rearrange("(p j) w -> p j w", j=PACK)

        nc.scalar.dma_start(out=q_raw[0][:], in_=q_rows(0))
        nc.sync.dma_start(out=rows[0:SCALE_ROWS, :], in_=k_scales.bitcast(I32).rearrange("o f t -> f o t"))
        nc.sync.dma_start(offsets[:], offs)
        nc.vector.memset(ls_rows[:], 0.0)
        nc.sync.dma_start(out=ls_rows[0:P:32, :], in_=ls[0].rearrange("(g i) one -> g (i one)", i=32))
        nc.sync.dma_start(out=words[:].bitcast(I32), in_=k_words[0].rearrange("p t b -> p (t b)").bitcast(I32))
        nc.sync.dma_start(out=pd_sb[:], in_=pd[0])
        nc.sync.dma_start(out=q_raw[1][:], in_=q_rows(1))
        nc.vector.memset(rows[32:64, :], 0)
        nc.vector.memset(rows[64:P, :], 0)
        nc.vector.memset(planes[:], 0)

        q_bf = [keep.tile([P, NQ, PACK], BF16, name="q_bf%d" % o, align_bytes=64) for o in range(PASSES)]
        q_codes = [keep.tile([P, NQ], U32, name="q_codes%d" % o, align_bytes=64) for o in range(PASSES)]
        q_scale = [
            keep.tile([P, NQ], U8, name="q_scale0", align_bytes=64),
            reuse.tile([P, NQ], U8, name="q_scale1", offset=2 * N, align_bytes=64),
        ]

        def round_q(o, first, last):
            nc.vector.tensor_copy(
                out=q_bf[o][:, first:last, :].rearrange("p (c i) j -> p c j i", i=4),
                in_=q_raw[o][:, :, first:last].rearrange("p j (c i) -> p c j i", i=4),
            )

        def quantize_q(o, first, last):
            nc.vector.quantize_mx(
                out=q_codes[o][:, first:last].bitcast(FP8X4),
                scales=q_scale[o][:, first:last],
                in_=q_bf[o][:, first:last, :].rearrange("p w j -> p (w j)"),
            )

        picked_rows = keep.tile([P, N], U8, name="picked_rows", align_bytes=DMA_ALIGN)
        nc.vector.tensor_copy(picked_rows[:], rows[:].bitcast(U8).indirect(offsets[:]))
        for quad in range(4):
            nc.sync.dma_start(
                out=planes[32 * quad : 32 * quad + 4, :], in_=picked_rows[8 * quad : 8 * quad + 8, :].bitcast(I32)
            )
        round_q(0, 0, NQ)
        ls_cols = keep.tile([P, 32], F32, name="ls_cols", align_bytes=64)
        nc.vector.transpose(out=ls_cols[:], in_=ls_rows[:])
        quantize_q(0, 0, NQ)

        log_pd = keep.tile([P, N], F32, name="log_pd")
        nc.scalar.activation(out=log_pd[:], in_=pd_sb[:], func=ACT.Ln)

        picked = [keep.tile([P, HALF], U32, name="picked%d" % h) for h in range(2)]
        for h in range(2):
            nc.vector.tensor_copy(picked[h][:], words[:].indirect(offsets[:, h * HALF // 16 : (h + 1) * HALF // 16]))

        banks = [psum.tile([P, CHUNK], F32, name="bank%d" % c) for c in range(CHUNKS)]
        first_codes = keep.tile([P, 2 * HALF], U8, name="k_first", align_bytes=64)
        early = reuse.tile([P, 2 * (HALF + CHUNK)], U8, name="k_early", offset=0, align_bytes=64)
        late = keep.tile([P, 2 * (CHUNKS - 1) * CHUNK], U8, name="k_late", tag="q_raw1", align_bytes=DMA_ALIGN)

        def codes(o, c, count=1):
            step = o * CHUNKS + c
            tile, at = (first_codes, step) if step < 2 else (early, step - 2) if step <= CHUNKS else (late, step - CHUNKS - 1)
            return tile[:, 2 * at * CHUNK : 2 * (at + count) * CHUNK]

        def split(o, first, end):
            h, at = divmod(first * CHUNK, HALF)
            pairs = picked[h][:].bitcast(U16).rearrange("p (n o) -> p o n", o=PASSES)
            nc.vector.tensor_copy(
                out=codes(o, first, end - first).bitcast(U16), in_=pairs[:, o, at : at + (end - first) * CHUNK]
            )

        def multiply(o, c):
            nc.tensor.matmul_mx(
                out=banks[c][:],
                lhsT=q_codes[o][:].bitcast(FP8X4),
                lhsT_scale=q_scale[o][:],
                rhs=codes(o, c).bitcast(FP4X4),
                rhs_scale=planes[:].bitcast(U8)[:, o * N + c * CHUNK : o * N + (c + 1) * CHUNK],
                start=(o == 0),
                stop=(o == PASSES - 1),
            )

        split(0, 0, 1)
        split(0, 1, 2)
        round_q(1, 0, NQ // 2)
        round_q(1, NQ // 2, Q_VECTOR)
        nc.scalar.copy(
            out=q_bf[1][:, Q_VECTOR:NQ, :].rearrange("p (c i) j -> p c j i", i=4),
            in_=q_raw[1][:, :, Q_VECTOR:NQ].rearrange("p j (c i) -> p c j i", i=4),
        )
        split(0, 2, CHUNKS)
        split(1, 0, 1)
        quantize_q(1, 0, NQ // 2)
        quantize_q(1, NQ // 2, NQ)
        split(1, 1, 2)
        split(1, 2, CHUNKS)
        for o in range(PASSES):
            for c in range(CHUNKS):
                multiply(o, c)

        log_ratio = keep.tile([P, N], F32, name="log_ratio")
        ratio = keep.tile([P, N], F32, name="ratio")
        result = [keep.tile([P, HALF], F32, name="result%d" % h, align_bytes=DMA_ALIGN) for h in range(2)]
        last = CHUNKS - 1
        pieces = [(c, 0, CHUNK) for c in range(last)] + [(last, 0, CHUNK // 2), (last, CHUNK // 2, CHUNK)]
        for c, a, b in pieces:
            cols = slice(c * CHUNK + a, c * CHUNK + b)
            nc.vector.scalar_tensor_tensor(
                out=log_ratio[:, cols], in0=banks[c][:, a:b], scalar=ls_cols[:, 0:1], in1=log_pd[:, cols],
                op0=ALU.subtract, op1=ALU.subtract,
            )
        for c, a, b in pieces:
            cols = slice(c * CHUNK + a, c * CHUNK + b)
            nc.scalar.activation(out=ratio[:, cols], in_=log_ratio[:, cols], func=ACT.Exp)
        for c, a, b in pieces:
            at = c % 2 * CHUNK
            nc.vector.tensor_scalar_min(
                out=result[c // 2][:, at + a : at + b], in0=ratio[:, c * CHUNK + a : c * CHUNK + b], scalar1=1.0
            )
            if b == CHUNK and c % 2 == 1:
                queue = nc.scalar if c == last else nc.sync
                queue.dma_start(out=out[0, :, (c - 1) * CHUNK : (c + 1) * CHUNK], in_=result[c // 2][:])
